import numpy as np, ml_dtypes
CORES = [89,94,345,350]
N = 4
import mx_ref
NC = 128
BF = ml_dtypes.bfloat16
def setup_inputs(rng):
    def f(*shape):
        return mx_ref.flush((rng.standard_normal(shape, dtype=np.float32) * np.exp2(rng.integers(-2, 3, shape[:-1] + (1,)))).astype(BF))
    return {"v": f(N, 128, 512), "p": f(N, 128, N * 4 * NC)}
def setup_inputs_blocks(rng):
    d = setup_inputs(rng)
    for k in ("v", "p"): d[k] = mx_ref.spread(d[k], rng, 1)
    return d
def setup_inputs_wide(rng):
    d = setup_inputs(rng)
    for k in ("v", "p"): d[k] = mx_ref.flush((d[k].astype(np.float32) * np.exp2(rng.integers(-8, 9, (N, 1, 1))).astype(np.float32)).astype(BF))
    return d
def setup_inputs_zeros(rng):
    d = setup_inputs(rng); v = d["p"].reshape(N, 128, -1, 4).copy()
    v[np.broadcast_to((rng.random((N, 1, v.shape[2], 1)) < 0.33), v.shape)] = 0
    d["p"] = v.reshape(d["p"].shape)
    return d
def reference(v, p):
    QV = [mx_ref.quantize(v[j]) for j in range(N)]
    y = np.zeros((N, 128, NC), np.float32)
    for r in range(N):
        for j in range(N):
            s = mx_ref.matmul(QV[j], mx_ref.quantize(p[r][:, 4 * NC * j:4 * NC * j + 4 * NC]))
            y[r] = s if j == 0 else y[r] + s
    return {"y": y}

@@ -1,0 +1,139 @@
+from concourse.bass import DstId, RemoteDMATransfer
+from concourse.mybir import dt
+
+N = 4
+W = 128
+HOSTS = 4
+
+SCRATCH = {
+    "vb": ("sbuf", [128, 4 * W], "bfloat16"),
+    "pb": ("sbuf", [128, 4 * W * N], "bfloat16"),
+    "vq": ("sbuf", [128, W * N], "float8_e4m3fn_x4"),
+    "vs": ("sbuf", [128, W * N], "uint8"),
+    "pq": ("sbuf", [128, W * N], "float8_e4m3fn_x4"),
+    "ps": ("sbuf", [128, W * N], "uint8"),
+    "acc": ("psum", [128, 512], "float32"),
+    "yb": ("sbuf", [128, W], "float32"),
+}
+SEMAPHORES = ["ldv", "ldp", "qv", "qp", "rs", "rc", "a0", "a1", "a2", "a3", "sent", "mm", "cp", "st"]
+
+
+def _bits(mask):
+    return [1 << e for e in range(mask.bit_length()) if mask >> e & 1]
+
+
+def _twin(topo, c, h):
+    return c + (h - topo.host(c)) * topo.CORES_PER_HOST
+
+
+def _plan(cores, topo):
+    plan = []
+    for s in cores:
+        near = [d for d in cores if d != s and topo.may_write(s, d)]
+        far = [d for d in cores if d != s and not topo.may_write(s, d)]
+        legs = []
+        for h in range(HOSTS):
+            t = _twin(topo, s, h)
+            if h == topo.host(s) or any(topo.host(d) == h for d in far):
+                continue
+            if not topo.may_write(s, t) or not all(topo.may_write(t, d) for d in far):
+                continue
+            if topo.rack(h) != topo.rack(topo.host(s)):
+                relay = t
+                dst = [d for d in far if topo.die(d) == topo.die(s)][0]
+            else:
+                taken = [_twin(topo, c, h) for c in cores]
+                base = t - t % topo.CORES_PER_CHIP
+                free = [c for c in range(base, base + topo.CORES_PER_CHIP)
+                        if topo.die(c) == topo.die(s) and c not in taken]
+                relay = max(free, key=lambda c: abs(c - t))
+                dst = [d for d in far if topo.die(d) != topo.die(s)][0]
+            legs.append((relay, dst))
+        plan.append((near, legs))
+    return plan
+
+
+def _count(mask):
+    return len(_bits(mask))
+
+
+def _relay_program(g, core, T, topo, j, dst):
+    sl = slice(j * W, (j + 1) * W)
+    rid, pid = topo.addr(dst, core)
+    mask = topo.mask(core, dst)
+    share = _count(topo.mask(T.cores[j], core)) // 2
+    g.wait_ge(T.sem.rs, share)
+    g.remote_dma(T.vs[:, sl], T.vs[:, sl], T.sem["a%d" % j], T.sem.sent, pid, rid, mask)
+    g.wait_ge(T.sem.rc, share)
+    g.remote_dma(T.vq[:, sl].bitcast(dt.uint8), T.vq[:, sl].bitcast(dt.uint8), T.sem["a%d" % j], T.sem.sent,
+                 pid, rid, mask)
+    g.wait_ge(T.sem.sent, 2 * _count(mask))
+
+
+def rank_program(g, core, T, topo):
+    cores = list(T.cores)
+    plan = _plan(cores, topo)
+    rank = T.rank_of(core)
+    if rank is None:
+        for j in range(N):
+            for relay, dst in plan[j][1]:
+                if relay == core:
+                    _relay_program(g, core, T, topo, j, dst)
+        return
+
+    sem = T.sem
+    near, legs = plan[rank]
+    sl = slice(rank * W, (rank + 1) * W)
+
+    g.sync.dma_start(T.vb[:], T.v[:]).then_inc(sem.ldv, 16)
+    g.sync.dma_start(T.pb[:], T.p[:]).then_inc(sem.ldp, 16)
+    g.vector.wait_ge(sem.ldv, 16)
+    g.vector.quantize_mx(T.vq[:, sl], T.vs[:, sl], T.vb[:]).then_inc(sem.qv, 1)
+    g.vector.wait_ge(sem.ldp, 16)
+    g.vector.quantize_mx(T.pq[:], T.ps[:], T.pb[:]).then_inc(sem.qp, 1)
+
+    off = topo.mask(core, legs[0][0])
+    for relay, _ in legs:
+        off &= topo.mask(core, relay)
+    eng = _bits(off)
+    shares = [sum(eng[k::len(legs)]) for k in range(len(legs))]
+    sent = 0
+    g.wait_ge(sem.qv, 1)
+    for arrive, src in ((sem.rs, T.vs[:, sl]), (sem.rc, T.vq[:, sl].bitcast(dt.uint8))):
+        trs = []
+        for (relay, _), m in zip(legs, shares):
+            rid, pid = topo.addr(relay, core)
+            trs.append(RemoteDMATransfer(dst_ids=[DstId(rid=rid, pnc=pid)], dma_engine_mask=m, remote_sem=arrive,
+                                         src=src, dst=src))
+            sent += _count(m)
+        g.remote_dma_fused(trs, local_sem=sem.sent)
+    for d in near:
+        rid, pid = topo.addr(d, core)
+        m = topo.mask(core, d) & ~off
+        for src in (T.vs[:, sl], T.vq[:, sl].bitcast(dt.uint8)):
+            g.remote_dma(src, src, sem["a%d" % rank], sem.sent, pid, rid, m)
+            sent += _count(m)
+    g.wait_ge(sem.sent, sent)
+
+    order = [(rank, None)]
+    for j in range(N):
+        if core in plan[j][0]:
+            order.append((j, 2 * _count(topo.mask(cores[j], core) & ~off)))
+    for j in range(N):
+        for relay, dst in plan[j][1]:
+            if dst == core:
+                order.append((j, 2 * _count(topo.mask(relay, core))))
+    g.tensor.wait_ge(sem.qv, 1)
+    g.tensor.wait_ge(sem.qp, 1)
+    for k, (j, need) in enumerate(order):
+        if need is not None:
+            g.tensor.wait_ge(sem["a%d" % j], need)
+        c = slice(j * W, (j + 1) * W)
+        g.tensor.matmul_mx(T.acc[:, 0:W], T.vq[:, c], T.vs[:, c], T.pq[:, c], T.ps[:, c],
+                           k == 0, k == len(order) - 1).then_inc(sem.mm, 1)
+
+    g.vector.wait_ge(sem.mm, len(order))
+    g.vector.tensor_copy(T.yb[:], T.acc[:, 0:W]).then_inc(sem.cp, 1)
+    g.sync.wait_ge(sem.cp, 1)
+    g.sync.dma_start(T.y[:], T.yb[:]).then_inc(sem.st, 16)
+    g.sync.wait_ge(sem.st, 16)

@@ -3,6 +3,7 @@ from concourse.mybir import dt
 
 N = 4
 W = 128
+Q = W // 4
 HOSTS = 4
 
 SCRATCH = {
@@ -22,16 +23,32 @@ def _bits(mask):
     return [1 << e for e in range(mask.bit_length()) if mask >> e & 1]
 
 
+def _count(mask):
+    return len(_bits(mask))
+
+
+def _deal(mask, k):
+    eng = _bits(mask)
+    return [sum(eng[i::k]) for i in range(k)]
+
+
+def _off(topo, core, dsts):
+    m = topo.mask(core, dsts[0])
+    for d in dsts:
+        m &= topo.mask(core, d)
+    return m
+
+
 def _twin(topo, c, h):
     return c + (h - topo.host(c)) * topo.CORES_PER_HOST
 
 
 def _plan(cores, topo):
     plan = []
-    for s in cores:
+    for j, s in enumerate(cores):
         near = [d for d in cores if d != s and topo.may_write(s, d)]
         far = [d for d in cores if d != s and not topo.may_write(s, d)]
-        legs = []
+        by_switch, by_cable = [], []
         for h in range(HOSTS):
             t = _twin(topo, s, h)
             if h == topo.host(s) or any(topo.host(d) == h for d in far):
@@ -39,35 +56,45 @@ def _plan(cores, topo):
             if not topo.may_write(s, t) or not all(topo.may_write(t, d) for d in far):
                 continue
             if topo.rack(h) != topo.rack(topo.host(s)):
-                relay = t
-                dst = [d for d in far if topo.die(d) == topo.die(s)][0]
+                by_cable.append(t)
             else:
                 taken = [_twin(topo, c, h) for c in cores]
                 base = t - t % topo.CORES_PER_CHIP
                 free = [c for c in range(base, base + topo.CORES_PER_CHIP)
                         if topo.die(c) == topo.die(s) and c not in taken]
-                relay = max(free, key=lambda c: abs(c - t))
-                dst = [d for d in far if topo.die(d) != topo.die(s)][0]
-            legs.append((relay, dst))
-        plan.append((near, legs))
+                by_switch += [min(free), max(free)]
+        c0, (s1, s2), lo = by_cable[0], by_switch, j * W
+        off = _off(topo, s, by_switch + by_cable)
+        half, rest = _deal(off, 2)
+        m1, m2 = _deal(rest, 2)
+        calls = [[(c0, False, lo, lo + W, half), (s1, True, lo, lo + Q, m1), (s2, True, lo + Q, lo + 2 * Q, m2)],
+                 [(c0, True, lo + 2 * Q, lo + W, off)]]
+        plan.append((near, far, calls))
     return plan
 
 
-def _count(mask):
-    return len(_bits(mask))
+def _view(T, codes, lo, hi):
+    return T.vq[:, lo:hi].bitcast(dt.uint8) if codes else T.vs[:, lo:hi]
 
 
-def _relay_program(g, core, T, topo, j, dst):
-    sl = slice(j * W, (j + 1) * W)
-    rid, pid = topo.addr(dst, core)
-    mask = topo.mask(core, dst)
-    share = _count(topo.mask(T.cores[j], core)) // 2
-    g.wait_ge(T.sem.rs, share)
-    g.remote_dma(T.vs[:, sl], T.vs[:, sl], T.sem["a%d" % j], T.sem.sent, pid, rid, mask)
-    g.wait_ge(T.sem.rc, share)
-    g.remote_dma(T.vq[:, sl].bitcast(dt.uint8), T.vq[:, sl].bitcast(dt.uint8), T.sem["a%d" % j], T.sem.sent,
-                 pid, rid, mask)
-    g.wait_ge(T.sem.sent, 2 * _count(mask))
+def _fused(g, core, T, topo, items):
+    trs = []
+    for d, ap, m, arrive in items:
+        rid, pid = topo.addr(d, core)
+        trs.append(RemoteDMATransfer(dst_ids=[DstId(rid=rid, pnc=pid)], dma_engine_mask=m, remote_sem=arrive,
+                                     src=ap, dst=ap))
+    g.remote_dma_fused(trs, local_sem=T.sem.sent)
+    return sum(_count(it[2]) for it in items)
+
+
+def _relay_program(g, core, T, topo, j, far, pieces):
+    masks = _deal(_off(topo, core, far), len(far))
+    sent = 0
+    for codes, lo, hi, m in pieces:
+        g.wait_ge(T.sem.rc if codes else T.sem.rs, _count(m))
+        sent += _fused(g, core, T, topo, [(d, _view(T, codes, lo, hi), md, T.sem["a%d" % j])
+                                          for d, md in zip(far, masks)])
+    g.wait_ge(T.sem.sent, sent)
 
 
 def rank_program(g, core, T, topo):
@@ -76,13 +103,14 @@ def rank_program(g, core, T, topo):
     rank = T.rank_of(core)
     if rank is None:
         for j in range(N):
-            for relay, dst in plan[j][1]:
-                if relay == core:
-                    _relay_program(g, core, T, topo, j, dst)
+            near, far, calls = plan[j]
+            pieces = [(codes, lo, hi, m) for call in calls for relay, codes, lo, hi, m in call if relay == core]
+            if pieces:
+                _relay_program(g, core, T, topo, j, far, pieces)
         return
 
     sem = T.sem
-    near, legs = plan[rank]
+    near, far, calls = plan[rank]
     sl = slice(rank * W, (rank + 1) * W)
 
     g.sync.dma_start(T.vb[:], T.v[:]).then_inc(sem.ldv, 16)
@@ -92,21 +120,15 @@ def rank_program(g, core, T, topo):
     g.vector.wait_ge(sem.ldp, 16)
     g.vector.quantize_mx(T.pq[:], T.ps[:], T.pb[:]).then_inc(sem.qp, 1)
 
-    off = topo.mask(core, legs[0][0])
-    for relay, _ in legs:
-        off &= topo.mask(core, relay)
-    eng = _bits(off)
-    shares = [sum(eng[k::len(legs)]) for k in range(len(legs))]
+    off = 0
+    for call in calls:
+        for piece in call:
+            off |= piece[4]
     sent = 0
     g.wait_ge(sem.qv, 1)
-    for arrive, src in ((sem.rs, T.vs[:, sl]), (sem.rc, T.vq[:, sl].bitcast(dt.uint8))):
-        trs = []
-        for (relay, _), m in zip(legs, shares):
-            rid, pid = topo.addr(relay, core)
-            trs.append(RemoteDMATransfer(dst_ids=[DstId(rid=rid, pnc=pid)], dma_engine_mask=m, remote_sem=arrive,
-                                         src=src, dst=src))
-            sent += _count(m)
-        g.remote_dma_fused(trs, local_sem=sem.sent)
+    for call in calls:
+        sent += _fused(g, core, T, topo, [(relay, _view(T, codes, lo, hi), m, sem.rc if codes else sem.rs)
+                                          for relay, codes, lo, hi, m in call])
     for d in near:
         rid, pid = topo.addr(d, core)
         m = topo.mask(core, d) & ~off
@@ -120,9 +142,12 @@ def rank_program(g, core, T, topo):
         if core in plan[j][0]:
             order.append((j, 2 * _count(topo.mask(cores[j], core) & ~off)))
     for j in range(N):
-        for relay, dst in plan[j][1]:
-            if dst == core:
-                order.append((j, 2 * _count(topo.mask(relay, core))))
+        if core in plan[j][1]:
+            fj, need = plan[j][1], 0
+            for call in plan[j][2]:
+                for piece in call:
+                    need += _count(_deal(_off(topo, piece[0], fj), len(fj))[fj.index(core)])
+            order.append((j, need))
     g.tensor.wait_ge(sem.qv, 1)
     g.tensor.wait_ge(sem.qp, 1)
     for k, (j, need) in enumerate(order):

from concourse.bass import DstId, RemoteDMATransfer
from concourse.mybir import dt

N = 4
W = 128
Q = W // 4
HOSTS = 4

SCRATCH = {
    "vb": ("sbuf", [128, 4 * W], "bfloat16"),
    "pb": ("sbuf", [128, 4 * W * N], "bfloat16"),
    "vq": ("sbuf", [128, W * N], "float8_e4m3fn_x4"),
    "vs": ("sbuf", [128, W * N], "uint8"),
    "pq": ("sbuf", [128, W * N], "float8_e4m3fn_x4"),
    "ps": ("sbuf", [128, W * N], "uint8"),
    "acc": ("psum", [128, 512], "float32"),
    "yb": ("sbuf", [128, W], "float32"),
}
SEMAPHORES = ["ldv", "ldp", "qv", "qp", "rs", "rc", "a0", "a1", "a2", "a3", "sent", "mm", "cp", "st"]


def _bits(mask):
    return [1 << e for e in range(mask.bit_length()) if mask >> e & 1]


def _count(mask):
    return len(_bits(mask))


def _deal(mask, k):
    eng = _bits(mask)
    return [sum(eng[i::k]) for i in range(k)]


def _off(topo, core, dsts):
    m = topo.mask(core, dsts[0])
    for d in dsts:
        m &= topo.mask(core, d)
    return m


def _twin(topo, c, h):
    return c + (h - topo.host(c)) * topo.CORES_PER_HOST


def _plan(cores, topo):
    plan = []
    for j, s in enumerate(cores):
        near = [d for d in cores if d != s and topo.may_write(s, d)]
        far = [d for d in cores if d != s and not topo.may_write(s, d)]
        by_switch, by_cable = [], []
        for h in range(HOSTS):
            t = _twin(topo, s, h)
            if h == topo.host(s) or any(topo.host(d) == h for d in far):
                continue
            if not topo.may_write(s, t) or not all(topo.may_write(t, d) for d in far):
                continue
            if topo.rack(h) != topo.rack(topo.host(s)):
                by_cable.append(t)
            else:
                taken = [_twin(topo, c, h) for c in cores]
                base = t - t % topo.CORES_PER_CHIP
                free = [c for c in range(base, base + topo.CORES_PER_CHIP)
                        if topo.die(c) == topo.die(s) and c not in taken]
                by_switch += [min(free), max(free)]
        c0, (s1, s2), lo = by_cable[0], by_switch, j * W
        off = _off(topo, s, by_switch + by_cable)
        half, rest = _deal(off, 2)
        m1, m2 = _deal(rest, 2)
        calls = [[(c0, False, lo, lo + W, half), (s1, True, lo, lo + Q, m1), (s2, True, lo + Q, lo + 2 * Q, m2)],
                 [(c0, True, lo + 2 * Q, lo + W, off)]]
        plan.append((near, far, calls))
    return plan


def _view(T, codes, lo, hi):
    return T.vq[:, lo:hi].bitcast(dt.uint8) if codes else T.vs[:, lo:hi]


def _fused(g, core, T, topo, items):
    trs = []
    for d, ap, m, arrive in items:
        rid, pid = topo.addr(d, core)
        trs.append(RemoteDMATransfer(dst_ids=[DstId(rid=rid, pnc=pid)], dma_engine_mask=m, remote_sem=arrive,
                                     src=ap, dst=ap))
    g.remote_dma_fused(trs, local_sem=T.sem.sent)
    return sum(_count(it[2]) for it in items)


def _relay_program(g, core, T, topo, j, far, pieces):
    masks = _deal(_off(topo, core, far), len(far))
    sent = 0
    for codes, lo, hi, m in pieces:
        g.wait_ge(T.sem.rc if codes else T.sem.rs, _count(m))
        sent += _fused(g, core, T, topo, [(d, _view(T, codes, lo, hi), md, T.sem["a%d" % j])
                                          for d, md in zip(far, masks)])
    g.wait_ge(T.sem.sent, sent)


def rank_program(g, core, T, topo):
    cores = list(T.cores)
    plan = _plan(cores, topo)
    rank = T.rank_of(core)
    if rank is None:
        for j in range(N):
            near, far, calls = plan[j]
            pieces = [(codes, lo, hi, m) for call in calls for relay, codes, lo, hi, m in call if relay == core]
            if pieces:
                _relay_program(g, core, T, topo, j, far, pieces)
        return

    sem = T.sem
    near, far, calls = plan[rank]
    sl = slice(rank * W, (rank + 1) * W)

    g.sync.dma_start(T.vb[:], T.v[:]).then_inc(sem.ldv, 16)
    g.sync.dma_start(T.pb[:], T.p[:]).then_inc(sem.ldp, 16)
    g.vector.wait_ge(sem.ldv, 16)
    g.vector.quantize_mx(T.vq[:, sl], T.vs[:, sl], T.vb[:]).then_inc(sem.qv, 1)
    g.vector.wait_ge(sem.ldp, 16)
    g.vector.quantize_mx(T.pq[:], T.ps[:], T.pb[:]).then_inc(sem.qp, 1)

    off = 0
    for call in calls:
        for piece in call:
            off |= piece[4]
    sent = 0
    g.wait_ge(sem.qv, 1)
    for call in calls:
        sent += _fused(g, core, T, topo, [(relay, _view(T, codes, lo, hi), m, sem.rc if codes else sem.rs)
                                          for relay, codes, lo, hi, m in call])
    for d in near:
        rid, pid = topo.addr(d, core)
        m = topo.mask(core, d) & ~off
        for src in (T.vs[:, sl], T.vq[:, sl].bitcast(dt.uint8)):
            g.remote_dma(src, src, sem["a%d" % rank], sem.sent, pid, rid, m)
            sent += _count(m)
    g.wait_ge(sem.sent, sent)

    order = [(rank, None)]
    for j in range(N):
        if core in plan[j][0]:
            order.append((j, 2 * _count(topo.mask(cores[j], core) & ~off)))
    for j in range(N):
        if core in plan[j][1]:
            fj, need = plan[j][1], 0
            for call in plan[j][2]:
                for piece in call:
                    need += _count(_deal(_off(topo, piece[0], fj), len(fj))[fj.index(core)])
            order.append((j, need))
    g.tensor.wait_ge(sem.qv, 1)
    g.tensor.wait_ge(sem.qp, 1)
    for k, (j, need) in enumerate(order):
        if need is not None:
            g.tensor.wait_ge(sem["a%d" % j], need)
        c = slice(j * W, (j + 1) * W)
        g.tensor.matmul_mx(T.acc[:, 0:W], T.vq[:, c], T.vs[:, c], T.pq[:, c], T.ps[:, c],
                           k == 0, k == len(order) - 1).then_inc(sem.mm, 1)

    g.vector.wait_ge(sem.mm, len(order))
    g.vector.tensor_copy(T.yb[:], T.acc[:, 0:W]).then_inc(sem.cp, 1)
    g.sync.wait_ge(sem.cp, 1)
    g.sync.dma_start(T.y[:], T.yb[:]).then_inc(sem.st, 16)
    g.sync.wait_ge(sem.st, 16)
